import numpy as np
import ml_dtypes


def mxq(x, axis, fmt="e4m3"):
    dtype, down = {"e4m3": (ml_dtypes.float8_e4m3fn, 7), "e5m2": (ml_dtypes.float8_e5m2, 14)}[fmt]
    v = np.moveaxis(np.asarray(x, np.float32).astype(ml_dtypes.bfloat16).astype(np.float64), axis, -1)
    blocks = v.reshape(v.shape[:-1] + (-1, 32))
    amax = np.abs(blocks).max(-1, keepdims=True)
    byte = np.maximum(np.where(amax > 0, np.frexp(amax)[1] - 1 + 127, 0) - down, 1)
    scale = np.exp2(byte - 127.0)
    codes = (blocks / scale).astype(np.float32).astype(dtype).astype(np.float64)
    return np.moveaxis((codes * scale).reshape(v.shape), -1, axis)


WIDE = False


def mx_kscale(k):
    if not WIDE:
        return np.ones(k)
    levels = np.array([10, -10, 5, -5, 0])
    if k % 512:
        return np.exp2(np.random.permutation(np.resize(levels, k // 32))).repeat(32)
    a = np.empty((k // 512, 16))
    for p in range(k // 512):
        a[p, :8] = np.random.permutation(np.resize(levels, 8))
        for g in range(8):
            far = levels[np.abs(levels - a[p, g]) >= 10]
            a[p, g + 8] = far[np.random.randint(len(far))]
    return np.exp2(a.ravel()).repeat(32)


def f64(x):
    return np.asarray(x).astype(np.float64)


def striped(idx):
    return np.tile(idx.reshape(-1, 16).T, (8, 1)).astype(np.uint16)


def unstriped(offs):
    return offs[:16].T.reshape(-1).astype(np.int64)


def striped8(idx):
    return np.concatenate([x.reshape(-1, 16).T for x in idx]).astype(np.uint16)


def runs(offs, k):
    lists = np.stack([offs[16 * r : 16 * r + 16].T.reshape(-1) for r in range(8)]).astype(np.int64)
    return lists[np.arange(k) % 512 // 64]


def pack_weight(w):
    k, n = w.shape
    w = f64(np.asarray(w, np.float32).astype(ml_dtypes.bfloat16)).reshape(k // 32, 32, n)
    amax = np.abs(w).max(1)
    byte = np.clip(np.where(amax > 0, np.frexp(amax)[1] - 1 + 127 - 7, 1), 1, 254)
    scaled = (w * np.exp2(127.0 - byte)[:, None, :]).reshape(k, n).astype(np.float32)
    words = np.ascontiguousarray(scaled.reshape(k // 512, 128, 4, n).transpose(0, 1, 3, 2)).astype(ml_dtypes.float8_e4m3fn).view(np.uint8)
    return words, np.ascontiguousarray(byte.astype(np.uint8).reshape(k // 512, 16, n))


def unpack_weight(words, scales):
    g, p, n, _ = words.shape
    vals = np.ascontiguousarray(words).view(ml_dtypes.float8_e4m3fn).astype(np.float64) * np.repeat(np.exp2(scales.astype(np.float64) - 127.0), 8, axis=1)[..., None]
    return vals.transpose(0, 1, 3, 2).reshape(g * 512, n)


def relu(v):
    return np.maximum(v, 0.0)


K, T, S, H, C, U = 512, 2048, 512, 512, 512, 1024


def setup_inputs():
    n = np.random.standard_normal
    s = mx_kscale(K)[:, None]
    packed_xT = pack_weight(n((K, T)) * s)
    return {
        "x_words": packed_xT[0],
        "x_scales": packed_xT[1],
        "w1": (n((K, H)) / np.sqrt(K) / s).astype(np.float32),
        "gs": (np.random.uniform(0.5, 1.5, (K, 1)) / s).astype(np.float32),
        "old": n((C, U)).astype(np.float32),
        "offs": striped(np.random.permutation(T)[:S]),
        "cand": striped(np.random.permutation(T)[:C]),
        "slot": striped8(np.stack([np.random.permutation(U)[:S] for _ in range(8)])),
    }


def reference(x_words, x_scales, w1, gs, old, offs, cand, slot):
    x_cand = unpack_weight(x_words, x_scales)[:, unstriped(cand)]
    xq = unpack_weight(x_words, x_scales)[:, unstriped(offs)]
    h = relu(mxq(f64(w1), 0, "e4m3").T @ xq)
    z = f64(gs) * h
    s = 0.0625 * ((x_cand.T @ mxq(z, 0, "e4m3")))
    nw = np.minimum(s, f64(old)[np.arange(C)[:, None], runs(slot, C)] + 0.5)
    out = f64(old).copy()
    out[np.arange(C)[:, None], runs(slot, C)] = nw
    return out

@@ -1,0 +1,147 @@
+from contextlib import ExitStack
+
+import concourse.mybir as mybir
+
+K, T, S, H, C, U = 512, 2048, 512, 512, 512, 1024
+FLOPS = 2 * K * H * S + 2 * K * C * S
+
+F32 = mybir.dt.float32
+BF16 = mybir.dt.bfloat16
+I32 = mybir.dt.int32
+U32 = mybir.dt.uint32
+U16 = mybir.dt.uint16
+U8 = mybir.dt.uint8
+FP8X4 = mybir.dt.float8_e4m3fn_x4
+ALU = mybir.AluOpType
+
+P = 128
+PACK = 4
+RUN = 8
+CHUNK = 128
+HALVES = 2
+
+
+def tile_picked_candput_none_p_kernel(tc, x_words, x_scales, w1, gs, old, offs, cand, slot, out):
+    nc = tc.nc
+    with ExitStack() as ctx:
+        keep = ctx.enter_context(tc.tile_pool(name="keep", bufs=1))
+        psum = ctx.enter_context(tc.psum_pool(name="psum", bufs=1))
+
+        offs_sb = keep.tile([P, S // 16], U16, name="offs_sb")
+        cand_sb = keep.tile([P, C // 16], U16, name="cand_sb")
+        slot_sb = keep.tile([P, S // 16], U16, name="slot_sb")
+        table_scales = keep.tile([P, T], U8, name="table_scales", align_bytes=64)
+        table_words = keep.tile([P, T], U32, name="table_words", align_bytes=64)
+        gs_sb = keep.tile([P, PACK], F32, name="gs_sb")
+        half = H // HALVES
+        w_raw = [keep.tile([P, PACK, half], F32, name=f"w_raw{a}", align_bytes=64) for a in range(HALVES)]
+        page = [keep.tile([P, U], F32, name=f"page{t}", align_bytes=64) for t in range(PACK)]
+
+        nc.vector.memset(table_scales[:].bitcast(I32), 0)
+        for q in range(4):
+            nc.scalar.dma_start(
+                out=table_scales[32 * q : 32 * q + 4, :].bitcast(I32),
+                in_=x_scales[0, 4 * q : 4 * q + 4, :].bitcast(I32),
+            )
+        nc.sync.dma_start(offs_sb[:], offs)
+        nc.sync.dma_start(cand_sb[:], cand)
+        nc.sync.dma_start(
+            out=table_words[:].bitcast(I32),
+            in_=x_words[0].rearrange("p n t -> p (n t)").bitcast(I32),
+        )
+        w_rows = w1.rearrange("(p j) c -> p j c", j=PACK)
+        for a in range(HALVES):
+            nc.sync.dma_start(out=w_raw[a][:], in_=w_rows[:, :, a * half : (a + 1) * half])
+        nc.scalar.dma_start(out=gs_sb[:], in_=gs.rearrange("(p t) o -> p (t o)", t=PACK))
+        nc.sync.dma_start(slot_sb[:], slot)
+        old_rows = old.rearrange("(q t r) u -> t q r u", t=PACK, r=RUN)
+        out_rows = out.rearrange("(q t r) u -> t q r u", t=PACK, r=RUN)
+        for t in range(PACK):
+            nc.sync.dma_start(out=page[t][:], in_=old_rows[t])
+
+        tok_scales = keep.tile([P, S], U8, name="tok_scales", align_bytes=64)
+        tok_words = keep.tile([P, S], U32, name="tok_words", align_bytes=64)
+        cand_scales_listed = keep.tile([P, C], U8, name="cand_scales_listed", align_bytes=64)
+        cand_scales = keep.tile([P, C], U8, name="cand_scales", align_bytes=64)
+        cand_words = keep.tile([P, C], U32, name="cand_words", align_bytes=64)
+        nc.vector.tensor_copy(tok_scales[:], table_scales[:].indirect(offs_sb[:]))
+        nc.vector.tensor_copy(cand_scales_listed[:], table_scales[:].indirect(cand_sb[:]))
+        nc.vector.tensor_copy(tok_words[:], table_words[:].indirect(offs_sb[:]))
+        nc.vector.tensor_copy(
+            cand_scales[:].bitcast(I32).rearrange("p (t q w) -> p t q w", t=PACK, w=RUN // 4),
+            cand_scales_listed[:].bitcast(I32).rearrange("p (q t w) -> p t q w", t=PACK, w=RUN // 4),
+        )
+        nc.vector.tensor_copy(
+            cand_words[:].rearrange("p (t q r) -> p q t r", t=PACK, r=RUN),
+            table_words[:].indirect(cand_sb[:]),
+        )
+
+        w_bf = keep.tile([P, H * PACK], BF16, name="w_bf", align_bytes=64)
+        w_dealt = w_bf[:].rearrange("p (t m j) -> p m t j", t=PACK, j=PACK)
+        m_half = P // HALVES
+        for a in range(HALVES):
+            nc.scalar.copy(
+                out=w_dealt[:, a * m_half : (a + 1) * m_half, :, :],
+                in_=w_raw[a][:].rearrange("p j (m t) -> p m t j", t=PACK),
+            )
+        w_words = keep.tile([P, H], U32, name="w_words", align_bytes=64)
+        w_scales = keep.tile([P, H], U8, name="w_scales", align_bytes=64)
+        nc.vector.quantize_mx(out=w_words[:].bitcast(FP8X4), scales=w_scales[:], in_=w_bf[:])
+
+        cap = [keep.tile([P, S], F32, name=f"cap{t}", align_bytes=64) for t in range(PACK)]
+
+        def fetch_cap(t):
+            nc.vector.tensor_scalar(cap[t][:], page[t][:].indirect(slot_sb[:]), 1.0, 0.5, ALU.mult, ALU.add)
+
+        fetch_cap(0)
+
+        z_bf = keep.tile([P, S * PACK], BF16, name="z_bf", align_bytes=64)
+        gs_rep = gs_sb[:].unsqueeze(1).to_broadcast([P, CHUNK, PACK])
+        for c in range(S // CHUNK):
+            cols = slice(c * CHUNK, (c + 1) * CHUNK)
+            h_bank = psum.tile([P, PACK, CHUNK], F32, name=f"h_bank{c}")
+            for t in range(PACK):
+                feats = slice(t * P, (t + 1) * P)
+                nc.tensor.matmul_mx(
+                    out=h_bank[:, t, :],
+                    lhsT=w_words[:, feats].bitcast(FP8X4),
+                    lhsT_scale=w_scales[:, feats],
+                    rhs=tok_words[:, cols].bitcast(FP8X4),
+                    rhs_scale=tok_scales[:, cols],
+                    start=True,
+                    stop=True,
+                )
+            nc.vector.scalar_tensor_tensor(
+                out=z_bf[:, c * CHUNK * PACK : (c + 1) * CHUNK * PACK].rearrange("p (n t) -> p n t", t=PACK),
+                in0=h_bank[:].rearrange("p t n -> p n t"),
+                scalar=0.0,
+                in1=gs_rep,
+                op0=ALU.max,
+                op1=ALU.mult,
+            )
+        z_words = keep.tile([P, S], U32, name="z_words", align_bytes=64)
+        z_scales = keep.tile([P, S], U8, name="z_scales", align_bytes=64)
+        nc.vector.quantize_mx(out=z_words[:].bitcast(FP8X4), scales=z_scales[:], in_=z_bf[:])
+
+        fetch_cap(1)
+
+        for t in range(PACK):
+            rows = slice(t * P, (t + 1) * P)
+            s_bank = psum.tile([P, S], F32, name=f"s_bank{t}")
+            nc.tensor.matmul_mx(
+                out=s_bank[:],
+                lhsT=cand_words[:, rows].bitcast(FP8X4),
+                lhsT_scale=cand_scales[:, rows],
+                rhs=z_words[:].bitcast(FP8X4),
+                rhs_scale=z_scales[:],
+                start=True,
+                stop=True,
+            )
+            new = keep.tile([P, S], F32, name=f"new{t}", align_bytes=64)
+            nc.vector.scalar_tensor_tensor(
+                out=new[:], in0=s_bank[:], scalar=0.0625, in1=cap[t][:], op0=ALU.mult, op1=ALU.min
+            )
+            if t + 2 < PACK:
+                fetch_cap(t + 2)
+            nc.vector.tensor_copy(page[t][:].indirect(slot_sb[:]), new[:])
+            nc.sync.dma_start(out=out_rows[t], in_=page[t][:])

@@ -38,13 +38,14 @@ def tile_picked_candput_none_p_kernel(tc, x_words, x_scales, w1, gs, old, offs, 
         page = [keep.tile([P, U], F32, name=f"page{t}", align_bytes=64) for t in range(PACK)]
 
         nc.vector.memset(table_scales[:].bitcast(I32), 0)
+        nc.sync.dma_start(offs_sb[:], offs)
+        nc.sync.dma_start(cand_sb[:], cand)
+        nc.sync.dma_start(slot_sb[:], slot)
         for q in range(4):
-            nc.scalar.dma_start(
+            nc.sync.dma_start(
                 out=table_scales[32 * q : 32 * q + 4, :].bitcast(I32),
                 in_=x_scales[0, 4 * q : 4 * q + 4, :].bitcast(I32),
             )
-        nc.sync.dma_start(offs_sb[:], offs)
-        nc.sync.dma_start(cand_sb[:], cand)
         nc.sync.dma_start(
             out=table_words[:].bitcast(I32),
             in_=x_words[0].rearrange("p n t -> p (n t)").bitcast(I32),
@@ -52,8 +53,7 @@ def tile_picked_candput_none_p_kernel(tc, x_words, x_scales, w1, gs, old, offs, 
         w_rows = w1.rearrange("(p j) c -> p j c", j=PACK)
         for a in range(HALVES):
             nc.sync.dma_start(out=w_raw[a][:], in_=w_rows[:, :, a * half : (a + 1) * half])
-        nc.scalar.dma_start(out=gs_sb[:], in_=gs.rearrange("(p t) o -> p (t o)", t=PACK))
-        nc.sync.dma_start(slot_sb[:], slot)
+        nc.sync.dma_start(out=gs_sb[:], in_=gs.rearrange("(p t) o -> p (t o)", t=PACK))
         old_rows = old.rearrange("(q t r) u -> t q r u", t=PACK, r=RUN)
         out_rows = out.rearrange("(q t r) u -> t q r u", t=PACK, r=RUN)
         for t in range(PACK):
@@ -125,7 +125,9 @@ def tile_picked_candput_none_p_kernel(tc, x_words, x_scales, w1, gs, old, offs, 
 
         fetch_cap(1)
 
-        for t in range(PACK):
+        new = [keep.tile([P, S], F32, name=f"new{t}", align_bytes=64) for t in range(PACK)]
+
+        def score(t):
             rows = slice(t * P, (t + 1) * P)
             s_bank = psum.tile([P, S], F32, name=f"s_bank{t}")
             nc.tensor.matmul_mx(
@@ -137,11 +139,15 @@ def tile_picked_candput_none_p_kernel(tc, x_words, x_scales, w1, gs, old, offs, 
                 start=True,
                 stop=True,
             )
-            new = keep.tile([P, S], F32, name=f"new{t}", align_bytes=64)
             nc.vector.scalar_tensor_tensor(
-                out=new[:], in0=s_bank[:], scalar=0.0625, in1=cap[t][:], op0=ALU.mult, op1=ALU.min
+                out=new[t][:], in0=s_bank[:], scalar=0.0625, in1=cap[t][:], op0=ALU.mult, op1=ALU.min
             )
+
+        score(0)
+        for t in range(PACK):
+            if t + 1 < PACK:
+                score(t + 1)
             if t + 2 < PACK:
                 fetch_cap(t + 2)
-            nc.vector.tensor_copy(page[t][:].indirect(slot_sb[:]), new[:])
+            nc.vector.tensor_copy(page[t][:].indirect(slot_sb[:]), new[t][:])
             nc.sync.dma_start(out=out_rows[t], in_=page[t][:])

@@ -16,7 +16,6 @@ ALU = mybir.AluOpType
 
 P = 128
 PACK = 4
-RUN = 8
 CHUNK = 128
 HALVES = 2
 
@@ -54,8 +53,8 @@ def tile_picked_candput_none_p_kernel(tc, x_words, x_scales, w1, gs, old, offs, 
         for a in range(HALVES):
             nc.sync.dma_start(out=w_raw[a][:], in_=w_rows[:, :, a * half : (a + 1) * half])
         nc.sync.dma_start(out=gs_sb[:], in_=gs.rearrange("(p t) o -> p (t o)", t=PACK))
-        old_rows = old.rearrange("(q t r) u -> t q r u", t=PACK, r=RUN)
-        out_rows = out.rearrange("(q t r) u -> t q r u", t=PACK, r=RUN)
+        old_rows = old.rearrange("(p t) u -> t p u", t=PACK)
+        out_rows = out.rearrange("(p t) u -> t p u", t=PACK)
         for t in range(PACK):
             nc.sync.dma_start(out=page[t][:], in_=old_rows[t])
 
@@ -63,17 +62,19 @@ def tile_picked_candput_none_p_kernel(tc, x_words, x_scales, w1, gs, old, offs, 
         tok_words = keep.tile([P, S], U32, name="tok_words", align_bytes=64)
         cand_scales_listed = keep.tile([P, C], U8, name="cand_scales_listed", align_bytes=64)
         cand_scales = keep.tile([P, C], U8, name="cand_scales", align_bytes=64)
+        cand_words_listed = keep.tile([P, C], U32, name="cand_words_listed", align_bytes=64)
         cand_words = keep.tile([P, C], U32, name="cand_words", align_bytes=64)
         nc.vector.tensor_copy(tok_scales[:], table_scales[:].indirect(offs_sb[:]))
         nc.vector.tensor_copy(cand_scales_listed[:], table_scales[:].indirect(cand_sb[:]))
         nc.vector.tensor_copy(tok_words[:], table_words[:].indirect(offs_sb[:]))
+        nc.vector.tensor_copy(cand_words_listed[:], table_words[:].indirect(cand_sb[:]))
         nc.vector.tensor_copy(
-            cand_scales[:].bitcast(I32).rearrange("p (t q w) -> p t q w", t=PACK, w=RUN // 4),
-            cand_scales_listed[:].bitcast(I32).rearrange("p (q t w) -> p t q w", t=PACK, w=RUN // 4),
+            cand_scales[:].rearrange("p (t m) -> p t m", t=PACK),
+            cand_scales_listed[:].rearrange("p (m t) -> p t m", t=PACK),
         )
         nc.vector.tensor_copy(
-            cand_words[:].rearrange("p (t q r) -> p q t r", t=PACK, r=RUN),
-            table_words[:].indirect(cand_sb[:]),
+            cand_words[:].rearrange("p (t m) -> p m t", t=PACK),
+            cand_words_listed[:].rearrange("p (m t) -> p m t", t=PACK),
         )
 
         w_bf = keep.tile([P, H * PACK], BF16, name="w_bf", align_bytes=64)

@@ -13,6 +13,7 @@ U16 = mybir.dt.uint16
 U8 = mybir.dt.uint8
 FP8X4 = mybir.dt.float8_e4m3fn_x4
 ALU = mybir.AluOpType
+ACT = mybir.ActivationFunctionType
 
 P = 128
 PACK = 4
@@ -36,10 +37,12 @@ def tile_picked_candput_none_p_kernel(tc, x_words, x_scales, w1, gs, old, offs, 
         w_raw = [keep.tile([P, PACK, half], F32, name=f"w_raw{a}", align_bytes=64) for a in range(HALVES)]
         page = [keep.tile([P, U], F32, name=f"page{t}", align_bytes=64) for t in range(PACK)]
 
+        old_rows = old.rearrange("(p t) u -> t p u", t=PACK)
+        out_rows = out.rearrange("(p t) u -> t p u", t=PACK)
         nc.vector.memset(table_scales[:].bitcast(I32), 0)
-        nc.sync.dma_start(offs_sb[:], offs)
         nc.sync.dma_start(cand_sb[:], cand)
-        nc.sync.dma_start(slot_sb[:], slot)
+        nc.sync.dma_start(offs_sb[:], offs)
+        nc.sync.dma_start(out=page[0][:, : U // 2], in_=old_rows[0][:, : U // 2])
         for q in range(4):
             nc.sync.dma_start(
                 out=table_scales[32 * q : 32 * q + 4, :].bitcast(I32),
@@ -52,10 +55,10 @@ def tile_picked_candput_none_p_kernel(tc, x_words, x_scales, w1, gs, old, offs, 
         w_rows = w1.rearrange("(p j) c -> p j c", j=PACK)
         for a in range(HALVES):
             nc.sync.dma_start(out=w_raw[a][:], in_=w_rows[:, :, a * half : (a + 1) * half])
+        nc.sync.dma_start(out=page[0][:, U // 2 :], in_=old_rows[0][:, U // 2 :])
+        nc.sync.dma_start(slot_sb[:], slot)
         nc.sync.dma_start(out=gs_sb[:], in_=gs.rearrange("(p t) o -> p (t o)", t=PACK))
-        old_rows = old.rearrange("(p t) u -> t p u", t=PACK)
-        out_rows = out.rearrange("(p t) u -> t p u", t=PACK)
-        for t in range(PACK):
+        for t in range(1, PACK):
             nc.sync.dma_start(out=page[t][:], in_=old_rows[t])
 
         tok_scales = keep.tile([P, S], U8, name="tok_scales", align_bytes=64)
@@ -64,14 +67,14 @@ def tile_picked_candput_none_p_kernel(tc, x_words, x_scales, w1, gs, old, offs, 
         cand_scales = keep.tile([P, C], U8, name="cand_scales", align_bytes=64)
         cand_words_listed = keep.tile([P, C], U32, name="cand_words_listed", align_bytes=64)
         cand_words = keep.tile([P, C], U32, name="cand_words", align_bytes=64)
-        nc.vector.tensor_copy(tok_scales[:], table_scales[:].indirect(offs_sb[:]))
         nc.vector.tensor_copy(cand_scales_listed[:], table_scales[:].indirect(cand_sb[:]))
-        nc.vector.tensor_copy(tok_words[:], table_words[:].indirect(offs_sb[:]))
-        nc.vector.tensor_copy(cand_words_listed[:], table_words[:].indirect(cand_sb[:]))
+        nc.vector.tensor_copy(tok_scales[:], table_scales[:].indirect(offs_sb[:]))
         nc.vector.tensor_copy(
             cand_scales[:].rearrange("p (t m) -> p t m", t=PACK),
             cand_scales_listed[:].rearrange("p (m t) -> p t m", t=PACK),
         )
+        nc.vector.tensor_copy(cand_words_listed[:], table_words[:].indirect(cand_sb[:]))
+        nc.vector.tensor_copy(tok_words[:], table_words[:].indirect(offs_sb[:]))
         nc.vector.tensor_copy(
             cand_words[:].rearrange("p (t m) -> p m t", t=PACK),
             cand_words_listed[:].rearrange("p (m t) -> p m t", t=PACK),
@@ -89,16 +92,18 @@ def tile_picked_candput_none_p_kernel(tc, x_words, x_scales, w1, gs, old, offs, 
         w_scales = keep.tile([P, H], U8, name="w_scales", align_bytes=64)
         nc.vector.quantize_mx(out=w_words[:].bitcast(FP8X4), scales=w_scales[:], in_=w_bf[:])
 
-        cap = [keep.tile([P, S], F32, name=f"cap{t}", align_bytes=64) for t in range(PACK)]
+        cap = [keep.tile([P, 2 * S], F32, name=f"cap{a}", align_bytes=64) for a in range(2)]
 
         def fetch_cap(t):
-            nc.vector.tensor_scalar(cap[t][:], page[t][:].indirect(slot_sb[:]), 1.0, 0.5, ALU.mult, ALU.add)
+            dst = cap[t // 2][:, (t % 2) * S : (t % 2 + 1) * S]
+            nc.vector.tensor_scalar(dst, page[t][:].indirect(slot_sb[:]), 1.0, 0.5, ALU.mult, ALU.add)
 
         fetch_cap(0)
+        fetch_cap(1)
 
         z_bf = keep.tile([P, S * PACK], BF16, name="z_bf", align_bytes=64)
         gs_rep = gs_sb[:].unsqueeze(1).to_broadcast([P, CHUNK, PACK])
-        for c in range(S // CHUNK):
+        for c in (0, 2, 1, 3):
             cols = slice(c * CHUNK, (c + 1) * CHUNK)
             h_bank = psum.tile([P, PACK, CHUNK], F32, name=f"h_bank{c}")
             for t in range(PACK):
@@ -112,43 +117,61 @@ def tile_picked_candput_none_p_kernel(tc, x_words, x_scales, w1, gs, old, offs, 
                     start=True,
                     stop=True,
                 )
-            nc.vector.scalar_tensor_tensor(
-                out=z_bf[:, c * CHUNK * PACK : (c + 1) * CHUNK * PACK].rearrange("p (n t) -> p n t", t=PACK),
-                in0=h_bank[:].rearrange("p t n -> p n t"),
-                scalar=0.0,
-                in1=gs_rep,
-                op0=ALU.max,
-                op1=ALU.mult,
-            )
+            z_chunk = z_bf[:, c * CHUNK * PACK : (c + 1) * CHUNK * PACK].rearrange("p (n t) -> p n t", t=PACK)
+            if c == 2:
+                h_sb = keep.tile([P, PACK, CHUNK], F32, name="h_sb", align_bytes=64)
+                z_planes = cap[1][:, S : S + PACK * CHUNK // 2].bitcast(BF16).rearrange("p (t n) -> p t n", t=PACK)
+                for t in range(0, PACK, 2):
+                    nc.scalar.activation(h_sb[:, t : t + 2, :], h_bank[:, t : t + 2, :], ACT.Relu)
+                for t in range(PACK):
+                    nc.scalar.activation(z_planes[:, t, :], h_sb[:, t, :], ACT.Copy, scale=gs_sb[:, t : t + 1])
+                nc.scalar.copy(out=z_chunk, in_=z_planes.rearrange("p t n -> p n t"))
+            else:
+                nc.vector.scalar_tensor_tensor(
+                    out=z_chunk,
+                    in0=h_bank[:].rearrange("p t n -> p n t"),
+                    scalar=0.0,
+                    in1=gs_rep,
+                    op0=ALU.max,
+                    op1=ALU.mult,
+                )
+        fetch_cap(2)
         z_words = keep.tile([P, S], U32, name="z_words", align_bytes=64)
         z_scales = keep.tile([P, S], U8, name="z_scales", align_bytes=64)
-        nc.vector.quantize_mx(out=z_words[:].bitcast(FP8X4), scales=z_scales[:], in_=z_bf[:])
-
-        fetch_cap(1)
-
-        new = [keep.tile([P, S], F32, name=f"new{t}", align_bytes=64) for t in range(PACK)]
-
-        def score(t):
-            rows = slice(t * P, (t + 1) * P)
-            s_bank = psum.tile([P, S], F32, name=f"s_bank{t}")
-            nc.tensor.matmul_mx(
-                out=s_bank[:],
-                lhsT=cand_words[:, rows].bitcast(FP8X4),
-                lhsT_scale=cand_scales[:, rows],
-                rhs=z_words[:].bitcast(FP8X4),
-                rhs_scale=z_scales[:],
-                start=True,
-                stop=True,
-            )
-            nc.vector.scalar_tensor_tensor(
-                out=new[t][:], in0=s_bank[:], scalar=0.0625, in1=cap[t][:], op0=ALU.mult, op1=ALU.min
+        for b in range(2):
+            cols = slice(b * (S // 2), (b + 1) * (S // 2))
+            nc.vector.quantize_mx(
+                out=z_words[:, cols].bitcast(FP8X4),
+                scales=z_scales[:, cols],
+                in_=z_bf[:, b * (S // 2) * PACK : (b + 1) * (S // 2) * PACK],
             )
 
-        score(0)
+        fetch_cap(3)
+
+        new = [keep.tile([P, 2, S], F32, name=f"new{a}", align_bytes=64) for a in range(2)]
+        for a in range(2):
+            for b in range(2):
+                cols = slice(b * (S // 2), (b + 1) * (S // 2))
+                s_bank = psum.tile([P, 2, S // 2], F32, name=f"s_bank{a}{b}")
+                for e in range(2):
+                    rows = slice((2 * a + e) * P, (2 * a + e + 1) * P)
+                    nc.tensor.matmul_mx(
+                        out=s_bank[:, e, :],
+                        lhsT=cand_words[:, rows].bitcast(FP8X4),
+                        lhsT_scale=cand_scales[:, rows],
+                        rhs=z_words[:, cols].bitcast(FP8X4),
+                        rhs_scale=z_scales[:, cols],
+                        start=True,
+                        stop=True,
+                    )
+                nc.vector.scalar_tensor_tensor(
+                    out=new[a][:, :, cols],
+                    in0=s_bank[:],
+                    scalar=0.0625,
+                    in1=cap[a][:].rearrange("p (e n) -> p e n", e=2)[:, :, cols],
+                    op0=ALU.mult,
+                    op1=ALU.min,
+                )
         for t in range(PACK):
-            if t + 1 < PACK:
-                score(t + 1)
-            if t + 2 < PACK:
-                fetch_cap(t + 2)
-            nc.vector.tensor_copy(page[t][:].indirect(slot_sb[:]), new[t][:])
+            nc.vector.tensor_copy(page[t][:].indirect(slot_sb[:]), new[t // 2][:, t % 2, :])
             nc.sync.dma_start(out=out_rows[t], in_=page[t][:])

@@ -18,6 +18,7 @@ ACT = mybir.ActivationFunctionType
 P = 128
 PACK = 4
 CHUNK = 128
+RUN = 4
 HALVES = 2
 
 
@@ -37,12 +38,12 @@ def tile_picked_candput_none_p_kernel(tc, x_words, x_scales, w1, gs, old, offs, 
         w_raw = [keep.tile([P, PACK, half], F32, name=f"w_raw{a}", align_bytes=64) for a in range(HALVES)]
         page = [keep.tile([P, U], F32, name=f"page{t}", align_bytes=64) for t in range(PACK)]
 
-        old_rows = old.rearrange("(p t) u -> t p u", t=PACK)
-        out_rows = out.rearrange("(p t) u -> t p u", t=PACK)
+        old_rows = old.rearrange("(q t r) u -> t q r u", t=PACK, r=RUN)
+        out_rows = out.rearrange("(q t r) u -> t q r u", t=PACK, r=RUN)
         nc.vector.memset(table_scales[:].bitcast(I32), 0)
         nc.sync.dma_start(cand_sb[:], cand)
         nc.sync.dma_start(offs_sb[:], offs)
-        nc.sync.dma_start(out=page[0][:, : U // 2], in_=old_rows[0][:, : U // 2])
+        nc.sync.dma_start(out=page[0][:, : U // 2], in_=old_rows[0][:, :, : U // 2])
         for q in range(4):
             nc.sync.dma_start(
                 out=table_scales[32 * q : 32 * q + 4, :].bitcast(I32),
@@ -55,7 +56,7 @@ def tile_picked_candput_none_p_kernel(tc, x_words, x_scales, w1, gs, old, offs, 
         w_rows = w1.rearrange("(p j) c -> p j c", j=PACK)
         for a in range(HALVES):
             nc.sync.dma_start(out=w_raw[a][:], in_=w_rows[:, :, a * half : (a + 1) * half])
-        nc.sync.dma_start(out=page[0][:, U // 2 :], in_=old_rows[0][:, U // 2 :])
+        nc.sync.dma_start(out=page[0][:, U // 2 :], in_=old_rows[0][:, :, U // 2 :])
         nc.sync.dma_start(slot_sb[:], slot)
         nc.sync.dma_start(out=gs_sb[:], in_=gs.rearrange("(p t) o -> p (t o)", t=PACK))
         for t in range(1, PACK):
@@ -65,19 +66,17 @@ def tile_picked_candput_none_p_kernel(tc, x_words, x_scales, w1, gs, old, offs, 
         tok_words = keep.tile([P, S], U32, name="tok_words", align_bytes=64)
         cand_scales_listed = keep.tile([P, C], U8, name="cand_scales_listed", align_bytes=64)
         cand_scales = keep.tile([P, C], U8, name="cand_scales", align_bytes=64)
-        cand_words_listed = keep.tile([P, C], U32, name="cand_words_listed", align_bytes=64)
         cand_words = keep.tile([P, C], U32, name="cand_words", align_bytes=64)
         nc.vector.tensor_copy(cand_scales_listed[:], table_scales[:].indirect(cand_sb[:]))
         nc.vector.tensor_copy(tok_scales[:], table_scales[:].indirect(offs_sb[:]))
         nc.vector.tensor_copy(
-            cand_scales[:].rearrange("p (t m) -> p t m", t=PACK),
-            cand_scales_listed[:].rearrange("p (m t) -> p t m", t=PACK),
+            cand_scales[:].bitcast(I32).rearrange("p (t q) -> p t q", t=PACK),
+            cand_scales_listed[:].bitcast(I32).rearrange("p (q t) -> p t q", t=PACK),
         )
-        nc.vector.tensor_copy(cand_words_listed[:], table_words[:].indirect(cand_sb[:]))
         nc.vector.tensor_copy(tok_words[:], table_words[:].indirect(offs_sb[:]))
         nc.vector.tensor_copy(
-            cand_words[:].rearrange("p (t m) -> p m t", t=PACK),
-            cand_words_listed[:].rearrange("p (m t) -> p m t", t=PACK),
+            cand_words[:].rearrange("p (t q r) -> p q t r", t=PACK, r=RUN),
+            table_words[:].indirect(cand_sb[:]),
         )
 
         w_bf = keep.tile([P, H * PACK], BF16, name="w_bf", align_bytes=64)

from contextlib import ExitStack

import concourse.mybir as mybir

K, T, S, H, C, U = 512, 2048, 512, 512, 512, 1024
FLOPS = 2 * K * H * S + 2 * K * C * S

F32 = mybir.dt.float32
BF16 = mybir.dt.bfloat16
I32 = mybir.dt.int32
U32 = mybir.dt.uint32
U16 = mybir.dt.uint16
U8 = mybir.dt.uint8
FP8X4 = mybir.dt.float8_e4m3fn_x4
ALU = mybir.AluOpType
ACT = mybir.ActivationFunctionType

P = 128
PACK = 4
CHUNK = 128
RUN = 4
HALVES = 2


def tile_picked_candput_none_p_kernel(tc, x_words, x_scales, w1, gs, old, offs, cand, slot, out):
    nc = tc.nc
    with ExitStack() as ctx:
        keep = ctx.enter_context(tc.tile_pool(name="keep", bufs=1))
        psum = ctx.enter_context(tc.psum_pool(name="psum", bufs=1))

        offs_sb = keep.tile([P, S // 16], U16, name="offs_sb")
        cand_sb = keep.tile([P, C // 16], U16, name="cand_sb")
        slot_sb = keep.tile([P, S // 16], U16, name="slot_sb")
        table_scales = keep.tile([P, T], U8, name="table_scales", align_bytes=64)
        table_words = keep.tile([P, T], U32, name="table_words", align_bytes=64)
        gs_sb = keep.tile([P, PACK], F32, name="gs_sb")
        half = H // HALVES
        w_raw = [keep.tile([P, PACK, half], F32, name=f"w_raw{a}", align_bytes=64) for a in range(HALVES)]
        page = [keep.tile([P, U], F32, name=f"page{t}", align_bytes=64) for t in range(PACK)]

        old_rows = old.rearrange("(q t r) u -> t q r u", t=PACK, r=RUN)
        out_rows = out.rearrange("(q t r) u -> t q r u", t=PACK, r=RUN)
        nc.vector.memset(table_scales[:].bitcast(I32), 0)
        nc.sync.dma_start(cand_sb[:], cand)
        nc.sync.dma_start(offs_sb[:], offs)
        nc.sync.dma_start(out=page[0][:, : U // 2], in_=old_rows[0][:, :, : U // 2])
        for q in range(4):
            nc.sync.dma_start(
                out=table_scales[32 * q : 32 * q + 4, :].bitcast(I32),
                in_=x_scales[0, 4 * q : 4 * q + 4, :].bitcast(I32),
            )
        nc.sync.dma_start(
            out=table_words[:].bitcast(I32),
            in_=x_words[0].rearrange("p n t -> p (n t)").bitcast(I32),
        )
        w_rows = w1.rearrange("(p j) c -> p j c", j=PACK)
        for a in range(HALVES):
            nc.sync.dma_start(out=w_raw[a][:], in_=w_rows[:, :, a * half : (a + 1) * half])
        nc.sync.dma_start(out=page[0][:, U // 2 :], in_=old_rows[0][:, :, U // 2 :])
        nc.sync.dma_start(slot_sb[:], slot)
        nc.sync.dma_start(out=gs_sb[:], in_=gs.rearrange("(p t) o -> p (t o)", t=PACK))
        for t in range(1, PACK):
            nc.sync.dma_start(out=page[t][:], in_=old_rows[t])

        tok_scales = keep.tile([P, S], U8, name="tok_scales", align_bytes=64)
        tok_words = keep.tile([P, S], U32, name="tok_words", align_bytes=64)
        cand_scales_listed = keep.tile([P, C], U8, name="cand_scales_listed", align_bytes=64)
        cand_scales = keep.tile([P, C], U8, name="cand_scales", align_bytes=64)
        cand_words = keep.tile([P, C], U32, name="cand_words", align_bytes=64)
        nc.vector.tensor_copy(cand_scales_listed[:], table_scales[:].indirect(cand_sb[:]))
        nc.vector.tensor_copy(tok_scales[:], table_scales[:].indirect(offs_sb[:]))
        nc.vector.tensor_copy(
            cand_scales[:].bitcast(I32).rearrange("p (t q) -> p t q", t=PACK),
            cand_scales_listed[:].bitcast(I32).rearrange("p (q t) -> p t q", t=PACK),
        )
        nc.vector.tensor_copy(tok_words[:], table_words[:].indirect(offs_sb[:]))
        nc.vector.tensor_copy(
            cand_words[:].rearrange("p (t q r) -> p q t r", t=PACK, r=RUN),
            table_words[:].indirect(cand_sb[:]),
        )

        w_bf = keep.tile([P, H * PACK], BF16, name="w_bf", align_bytes=64)
        w_dealt = w_bf[:].rearrange("p (t m j) -> p m t j", t=PACK, j=PACK)
        m_half = P // HALVES
        for a in range(HALVES):
            nc.scalar.copy(
                out=w_dealt[:, a * m_half : (a + 1) * m_half, :, :],
                in_=w_raw[a][:].rearrange("p j (m t) -> p m t j", t=PACK),
            )
        w_words = keep.tile([P, H], U32, name="w_words", align_bytes=64)
        w_scales = keep.tile([P, H], U8, name="w_scales", align_bytes=64)
        nc.vector.quantize_mx(out=w_words[:].bitcast(FP8X4), scales=w_scales[:], in_=w_bf[:])

        cap = [keep.tile([P, 2 * S], F32, name=f"cap{a}", align_bytes=64) for a in range(2)]

        def fetch_cap(t):
            dst = cap[t // 2][:, (t % 2) * S : (t % 2 + 1) * S]
            nc.vector.tensor_scalar(dst, page[t][:].indirect(slot_sb[:]), 1.0, 0.5, ALU.mult, ALU.add)

        fetch_cap(0)
        fetch_cap(1)

        z_bf = keep.tile([P, S * PACK], BF16, name="z_bf", align_bytes=64)
        gs_rep = gs_sb[:].unsqueeze(1).to_broadcast([P, CHUNK, PACK])
        for c in (0, 2, 1, 3):
            cols = slice(c * CHUNK, (c + 1) * CHUNK)
            h_bank = psum.tile([P, PACK, CHUNK], F32, name=f"h_bank{c}")
            for t in range(PACK):
                feats = slice(t * P, (t + 1) * P)
                nc.tensor.matmul_mx(
                    out=h_bank[:, t, :],
                    lhsT=w_words[:, feats].bitcast(FP8X4),
                    lhsT_scale=w_scales[:, feats],
                    rhs=tok_words[:, cols].bitcast(FP8X4),
                    rhs_scale=tok_scales[:, cols],
                    start=True,
                    stop=True,
                )
            z_chunk = z_bf[:, c * CHUNK * PACK : (c + 1) * CHUNK * PACK].rearrange("p (n t) -> p n t", t=PACK)
            if c == 2:
                h_sb = keep.tile([P, PACK, CHUNK], F32, name="h_sb", align_bytes=64)
                z_planes = cap[1][:, S : S + PACK * CHUNK // 2].bitcast(BF16).rearrange("p (t n) -> p t n", t=PACK)
                for t in range(0, PACK, 2):
                    nc.scalar.activation(h_sb[:, t : t + 2, :], h_bank[:, t : t + 2, :], ACT.Relu)
                for t in range(PACK):
                    nc.scalar.activation(z_planes[:, t, :], h_sb[:, t, :], ACT.Copy, scale=gs_sb[:, t : t + 1])
                nc.scalar.copy(out=z_chunk, in_=z_planes.rearrange("p t n -> p n t"))
            else:
                nc.vector.scalar_tensor_tensor(
                    out=z_chunk,
                    in0=h_bank[:].rearrange("p t n -> p n t"),
                    scalar=0.0,
                    in1=gs_rep,
                    op0=ALU.max,
                    op1=ALU.mult,
                )
        fetch_cap(2)
        z_words = keep.tile([P, S], U32, name="z_words", align_bytes=64)
        z_scales = keep.tile([P, S], U8, name="z_scales", align_bytes=64)
        for b in range(2):
            cols = slice(b * (S // 2), (b + 1) * (S // 2))
            nc.vector.quantize_mx(
                out=z_words[:, cols].bitcast(FP8X4),
                scales=z_scales[:, cols],
                in_=z_bf[:, b * (S // 2) * PACK : (b + 1) * (S // 2) * PACK],
            )

        fetch_cap(3)

        new = [keep.tile([P, 2, S], F32, name=f"new{a}", align_bytes=64) for a in range(2)]
        for a in range(2):
            for b in range(2):
                cols = slice(b * (S // 2), (b + 1) * (S // 2))
                s_bank = psum.tile([P, 2, S // 2], F32, name=f"s_bank{a}{b}")
                for e in range(2):
                    rows = slice((2 * a + e) * P, (2 * a + e + 1) * P)
                    nc.tensor.matmul_mx(
                        out=s_bank[:, e, :],
                        lhsT=cand_words[:, rows].bitcast(FP8X4),
                        lhsT_scale=cand_scales[:, rows],
                        rhs=z_words[:, cols].bitcast(FP8X4),
                        rhs_scale=z_scales[:, cols],
                        start=True,
                        stop=True,
                    )
                nc.vector.scalar_tensor_tensor(
                    out=new[a][:, :, cols],
                    in0=s_bank[:],
                    scalar=0.0625,
                    in1=cap[a][:].rearrange("p (e n) -> p e n", e=2)[:, :, cols],
                    op0=ALU.mult,
                    op1=ALU.min,
                )
        for t in range(PACK):
            nc.vector.tensor_copy(page[t][:].indirect(slot_sb[:]), new[t // 2][:, t % 2, :])
            nc.sync.dma_start(out=out_rows[t], in_=page[t][:])
